import numpy as np
import ml_dtypes


def mxq(x, axis, fmt="e4m3"):
    dtype, down = {"e4m3": (ml_dtypes.float8_e4m3fn, 7), "e5m2": (ml_dtypes.float8_e5m2, 14)}[fmt]
    v = np.moveaxis(np.asarray(x, np.float32).astype(ml_dtypes.bfloat16).astype(np.float64), axis, -1)
    blocks = v.reshape(v.shape[:-1] + (-1, 32))
    amax = np.abs(blocks).max(-1, keepdims=True)
    byte = np.maximum(np.where(amax > 0, np.frexp(amax)[1] - 1 + 127, 0) - down, 1)
    scale = np.exp2(byte - 127.0)
    codes = (blocks / scale).astype(np.float32).astype(dtype).astype(np.float64)
    return np.moveaxis((codes * scale).reshape(v.shape), -1, axis)


WIDE = False


def mx_kscale(k):
    if not WIDE:
        return np.ones(k)
    levels = np.array([24, -24, 12, -12, 0])
    if k % 512:
        return np.exp2(np.random.permutation(np.resize(levels, k // 32))).repeat(32)
    a = np.empty((k // 512, 16))
    for p in range(k // 512):
        a[p, :8] = np.random.permutation(np.resize(levels, 8))
        for g in range(8):
            far = levels[np.abs(levels - a[p, g]) >= 10]
            a[p, g + 8] = far[np.random.randint(len(far))]
    return np.exp2(a.ravel()).repeat(32)


def f64(x):
    return np.asarray(x).astype(np.float64)


def striped8(idx):
    return np.concatenate([v.reshape(-1, 16).T for v in idx]).astype(np.uint16)


def unstriped8(offs):
    return np.stack([offs[16 * g:16 * g + 16].T.reshape(-1) for g in range(8)]).astype(np.int64)


E2M1 = np.array([0.0, 0.5, 1.0, 1.5, 2.0, 3.0, 4.0, 6.0, -0.0, -0.5, -1.0, -1.5, -2.0, -3.0, -4.0, -6.0])


def pack_weight(w, fmt):
    k, n = w.shape
    w = f64(np.asarray(w, np.float32).astype(ml_dtypes.bfloat16)).reshape(k // 32, 32, n)
    amax = np.abs(w).max(1)
    if fmt == "e4m3":
        byte = np.frexp(amax)[1] - 1 + 127 - 7
    else:
        mant, ex = np.frexp(amax / 6.0)
        byte = np.where(mant > 0.5, ex, ex - 1) + 127
    byte = np.clip(np.where(amax > 0, byte, 1), 1, 254)
    scaled = (w * np.exp2(127.0 - byte)[:, None, :]).reshape(k, n).astype(np.float32)
    by_word = np.ascontiguousarray(scaled.reshape(k // 512, 128, 4, n).transpose(0, 1, 3, 2))
    if fmt == "e4m3":
        words = by_word.astype(ml_dtypes.float8_e4m3fn).view(np.uint8)
    else:
        c = by_word.astype(ml_dtypes.float4_e2m1fn).view(np.uint8) & 0xF
        words = (c[..., 0::2] | (c[..., 1::2] << 4)).reshape(k // 512, 128, 2 * n)
    return np.ascontiguousarray(words), np.ascontiguousarray(byte.astype(np.uint8).reshape(k // 512, 16, n))


def unpack_weight(words, scales, fmt):
    g, _, n = scales.shape
    words = np.ascontiguousarray(words).reshape(g, 128, n, -1)
    if fmt == "e4m3":
        vals = words.view(ml_dtypes.float8_e4m3fn).astype(np.float64)
    else:
        nib = np.empty((g, 128, n, 4), np.uint8)
        nib[..., 0::2] = words & 0xF
        nib[..., 1::2] = words >> 4
        vals = E2M1[nib]
    vals = vals * np.repeat(np.exp2(scales.astype(np.float64) - 127.0), 8, axis=1)[..., None]
    return vals.transpose(0, 1, 3, 2).reshape(g * 512, n)


def gelu(f):
    return 0.5 * f * (1.0 + np.tanh(np.sqrt(2.0 / np.pi) * (f + 0.044715 * f**3)))


K, N, T, J = 512, 512, 2048, 512


def setup_inputs():
    n = np.random.standard_normal
    s = mx_kscale(K)[:, None]
    p_w = pack_weight(n((K, N)) / np.sqrt(K) / s, "e2m1")
    return {
        "xT": (n((K, T)) * s).astype(np.float32),
        "wgt": np.repeat(np.random.uniform(0.5, 2.0, (8, 3 * J)), 16, axis=0).astype(np.float32),
        "w_words": p_w[0],
        "w_scales": p_w[1],
        "b": (0.3 * n(N)).astype(np.float32),
        "offs": striped8(np.stack([np.concatenate([np.random.permutation(T)[:J] for _ in range(3)]) for _ in range(8)])),
    }


def reference(xT, wgt, w_words, w_scales, b, offs):
    idx = unstriped8(offs)
    rows = np.arange(K)
    xg = f64(wgt)[rows // 4 % 128] * f64(xT)[rows[:, None], idx[rows % 512 // 64]]
    xT_ = mxq(xg, 0, "e4m3").reshape(K, 3, J)
    w_ = unpack_weight(w_words, w_scales, "e2m1")
    a0 = w_.T @ xT_[:, 0]
    a1 = w_.T @ xT_[:, 1]
    a2 = w_.T @ xT_[:, 2]
    return gelu(np.maximum(np.maximum(a0, a1), a2) + f64(b)[:, None])

@@ -1,0 +1,156 @@
+from contextlib import ExitStack
+
+import concourse.mybir as mybir
+
+K, N, T, J = 512, 512, 2048, 512
+PICKS = 3
+FLOPS = 2 * K * N * J * PICKS
+
+F32 = mybir.dt.float32
+BF16 = mybir.dt.bfloat16
+I32 = mybir.dt.int32
+U32 = mybir.dt.uint32
+U16 = mybir.dt.uint16
+U8 = mybir.dt.uint8
+FP8X4 = mybir.dt.float8_e4m3fn_x4
+FP4X4 = mybir.dt.float4_e2m1fn_x4
+MULT = mybir.AluOpType.mult
+MAX = mybir.AluOpType.max
+GELU = mybir.ActivationFunctionType.Gelu_apprx_tanh
+
+P = 128
+PACK = 4
+GROUP = 16
+CH = 128
+NCH = J // CH
+MT = N // P
+HEAD = 256
+
+
+def tile_list_max_gelu_kernel(tc, xT, wgt, w_words, w_scales, b, offs, out):
+    nc = tc.nc
+    with ExitStack() as ctx:
+        keep = ctx.enter_context(tc.tile_pool(name="keep", bufs=1))
+        psum = ctx.enter_context(tc.psum_pool(name="psum", bufs=1))
+
+        offsets = keep.tile([P, PICKS * J // GROUP], U16, name="offsets")
+        planes = [keep.tile([P, T], F32, name=f"plane{t}") for t in range(PACK)]
+        weights = [keep.tile([P, J], F32, name=f"wgt{c}") for c in range(PICKS)]
+        w_codes = keep.tile([P, 2 * N], U8, name="w_codes", align_bytes=64)
+        w_plane = keep.tile([P, N], U8, name="w_plane", align_bytes=64)
+        bias = keep.tile([P, MT], F32, name="bias")
+        warm = keep.tile([P, 2], F32, name="warm")
+
+        nc.vector.memset(warm[:, 0:1], 0.0)
+        nc.scalar.activation(warm[:, 1:2], warm[:, 0:1], GELU)
+        nc.vector.memset(w_plane[:].bitcast(I32), 0)
+
+        x_planes = xT.rearrange("(p t) n -> t p n", t=PACK)
+        nc.sync.dma_start(offsets[:], offs)
+        nc.sync.dma_start(weights[0][:, 0:HEAD], wgt[:, 0:HEAD])
+        nc.sync.dma_start(planes[0][:], x_planes[0])
+        nc.sync.dma_start(weights[0][:, HEAD:J], wgt[:, HEAD:J])
+        nc.sync.dma_start(weights[1][:], wgt[:, J : 2 * J])
+        nc.sync.dma_start(weights[2][:], wgt[:, 2 * J : 3 * J])
+        for t in range(1, PACK):
+            nc.sync.dma_start(planes[t][:], x_planes[t])
+        nc.sync.dma_start(w_codes[:].bitcast(I32), w_words[0].bitcast(I32))
+        for q in range(4):
+            nc.sync.dma_start(w_plane[32 * q : 32 * q + 4, :].bitcast(I32), w_scales[0, 4 * q : 4 * q + 4, :].bitcast(I32))
+        with nc.allow_non_contiguous_dma(reason="one bias value a partition"):
+            nc.sync.dma_start(bias[:], b.rearrange("(m p) -> p m", p=P))
+
+        early = [keep.tile([P, 2, J], F32, name=f"early{c}") for c in range(PICKS)]
+        late = {(h, c): keep.tile([P, 2, 2 * CH], F32, name=f"late{h}_{c}") for h in range(NCH // 2) for c in range(PICKS)}
+        rounded = [keep.tile([P, J, PACK], BF16, name=f"rounded{c}", align_bytes=64) for c in range(PICKS)]
+        codes = [keep.tile([P, J], U32, name=f"codes{c}", align_bytes=64) for c in range(PICKS)]
+        scales = [keep.tile([P, J], U8, name=f"scales{c}", align_bytes=64) for c in range(PICKS)]
+        first = [keep.tile([P, MT * CH], F32, name=f"first{q}") for q in range(NCH)]
+        pooled2 = [keep.tile([P, MT * CH], F32, name=f"pooled2_{q}") for q in range(NCH)]
+        pooled3 = [keep.tile([P, MT * CH], F32, name=f"pooled3_{q}") for q in range(NCH)]
+        result = [keep.tile([P, MT, CH], F32, name=f"result{q}") for q in range(NCH)]
+        out_view = out.rearrange("(m p) j -> p m j", p=P)
+        acc = {}
+
+        def gather(dst, t, c, j0, width):
+            col = (c * J + j0) // GROUP
+            nc.vector.tensor_tensor(
+                dst, planes[t][:].indirect(offsets[:, col : col + width // GROUP]), weights[c][:, j0 : j0 + width], MULT
+            )
+
+        def gather2(h, c):
+            gather(late[h, c][:, 0, :], 2, c, 2 * h * CH, 2 * CH)
+
+        def gather3(q, c):
+            s = slice(q % 2 * CH, (q % 2 + 1) * CH)
+            gather(late[q // 2, c][:, 1, s], 3, c, q * CH, CH)
+            nc.scalar.copy(rounded[c][:, q * CH : (q + 1) * CH, 2:4], late[q // 2, c][:, :, s].rearrange("p t j -> p j t"))
+
+        def project(q):
+            cols = slice(q * CH, (q + 1) * CH)
+            for c in range(PICKS):
+                nc.vector.quantize_mx(
+                    out=codes[c][:, cols].bitcast(FP8X4),
+                    scales=scales[c][:, cols],
+                    in_=rounded[c][:, cols, :].rearrange("p j t -> p (j t)"),
+                )
+                acc[q, c] = psum.tile([P, MT * CH], F32, name=f"acc{c}", bufs=2 if c == 0 else 3)
+                for m in range(MT):
+                    nc.tensor.matmul_mx(
+                        out=acc[q, c][:, m * CH : (m + 1) * CH],
+                        lhsT=w_codes[:, 2 * m * P : 2 * (m + 1) * P].bitcast(FP4X4),
+                        lhsT_scale=w_plane[:, m * P : (m + 1) * P],
+                        rhs=codes[c][:, cols].bitcast(FP8X4),
+                        rhs_scale=scales[c][:, cols],
+                        start=True,
+                        stop=True,
+                    )
+                if c == 0:
+                    nc.scalar.copy(first[q][:], acc[q, 0][:])
+
+        def max_a(q, m0=0, m1=MT):
+            s = slice(m0 * CH, m1 * CH)
+            nc.vector.tensor_tensor(pooled2[q][:, s], acc[q, 1][:, s], first[q][:, s], MAX)
+
+        def max_b(q, m0=0, m1=MT, queue=nc.sync):
+            s = slice(m0 * CH, m1 * CH)
+            nc.vector.tensor_tensor(pooled3[q][:, s], acc[q, 2][:, s], pooled2[q][:, s], MAX)
+            for m in range(m0, m1):
+                nc.scalar.activation(result[q][:, m, :], pooled3[q][:, m * CH : (m + 1) * CH], GELU, bias=bias[:, m : m + 1])
+            queue.dma_start(out_view[:, m0:m1, q * CH : (q + 1) * CH], result[q][:, m0:m1, :])
+
+        gather(early[0][:, 0, 0:HEAD], 0, 0, 0, HEAD)
+        gather(early[0][:, 0, HEAD:J], 0, 0, HEAD, J - HEAD)
+        for c in range(1, PICKS):
+            gather(early[c][:, 0, :], 0, c, 0, J)
+        for c in range(PICKS):
+            gather(early[c][:, 1, :], 1, c, 0, J)
+            nc.scalar.copy(rounded[c][:, :, 0:2], early[c][:].rearrange("p t j -> p j t"))
+
+        for c in range(PICKS):
+            gather2(0, c)
+        for c in range(PICKS):
+            gather3(0, c)
+        for c in range(PICKS):
+            gather3(1, c)
+        project(0)
+        for c in range(PICKS):
+            gather2(1, c)
+            gather3(2, c)
+        max_a(0)
+        project(1)
+        max_b(0)
+        gather3(3, 0)
+        project(2)
+        gather3(3, 1)
+        max_a(1)
+        gather3(3, 2)
+        max_b(1)
+        max_a(2)
+        project(3)
+        max_b(2)
+        max_a(3, 0, 2)
+        max_a(3, 2, 4)
+        max_b(3, 0, 2)
+        max_b(3, 2, 3)
+        max_b(3, 3, 4, nc.scalar)

@@ -21,10 +21,13 @@ GELU = mybir.ActivationFunctionType.Gelu_apprx_tanh
 P = 128
 PACK = 4
 GROUP = 16
-CH = 128
-NCH = J // CH
+HALF = J // 2
 MT = N // P
-HEAD = 256
+ENTRIES = PICKS * J
+FIRST_CUTS = [0, 256, 768, ENTRIES]
+PIECES = [(h, c) for h in range(2) for c in range(PICKS)]
+CELL = [0, 1, 2, 3, 0, 2]
+BANKS = [0, 2, 4, 6, 0, 2]
 
 
 def tile_list_max_gelu_kernel(tc, xT, wgt, w_words, w_scales, b, offs, out):
@@ -33,9 +36,9 @@ def tile_list_max_gelu_kernel(tc, xT, wgt, w_words, w_scales, b, offs, out):
         keep = ctx.enter_context(tc.tile_pool(name="keep", bufs=1))
         psum = ctx.enter_context(tc.psum_pool(name="psum", bufs=1))
 
-        offsets = keep.tile([P, PICKS * J // GROUP], U16, name="offsets")
+        offsets = keep.tile([P, ENTRIES // GROUP], U16, name="offsets")
         planes = [keep.tile([P, T], F32, name=f"plane{t}") for t in range(PACK)]
-        weights = [keep.tile([P, J], F32, name=f"wgt{c}") for c in range(PICKS)]
+        weights = keep.tile([P, ENTRIES], F32, name="weights")
         w_codes = keep.tile([P, 2 * N], U8, name="w_codes", align_bytes=64)
         w_plane = keep.tile([P, N], U8, name="w_plane", align_bytes=64)
         bias = keep.tile([P, MT], F32, name="bias")
@@ -46,12 +49,12 @@ def tile_list_max_gelu_kernel(tc, xT, wgt, w_words, w_scales, b, offs, out):
         nc.vector.memset(w_plane[:].bitcast(I32), 0)
 
         x_planes = xT.rearrange("(p t) n -> t p n", t=PACK)
+        cuts = [slice(lo, hi) for lo, hi in zip(FIRST_CUTS, FIRST_CUTS[1:])]
         nc.sync.dma_start(offsets[:], offs)
-        nc.sync.dma_start(weights[0][:, 0:HEAD], wgt[:, 0:HEAD])
+        nc.sync.dma_start(weights[:, cuts[0]], wgt[:, cuts[0]])
         nc.sync.dma_start(planes[0][:], x_planes[0])
-        nc.sync.dma_start(weights[0][:, HEAD:J], wgt[:, HEAD:J])
-        nc.sync.dma_start(weights[1][:], wgt[:, J : 2 * J])
-        nc.sync.dma_start(weights[2][:], wgt[:, 2 * J : 3 * J])
+        for cut in cuts[1:]:
+            nc.sync.dma_start(weights[:, cut], wgt[:, cut])
         for t in range(1, PACK):
             nc.sync.dma_start(planes[t][:], x_planes[t])
         nc.sync.dma_start(w_codes[:].bitcast(I32), w_words[0].bitcast(I32))
@@ -60,97 +63,98 @@ def tile_list_max_gelu_kernel(tc, xT, wgt, w_words, w_scales, b, offs, out):
         with nc.allow_non_contiguous_dma(reason="one bias value a partition"):
             nc.sync.dma_start(bias[:], b.rearrange("(m p) -> p m", p=P))
 
-        early = [keep.tile([P, 2, J], F32, name=f"early{c}") for c in range(PICKS)]
-        late = {(h, c): keep.tile([P, 2, 2 * CH], F32, name=f"late{h}_{c}") for h in range(NCH // 2) for c in range(PICKS)}
-        rounded = [keep.tile([P, J, PACK], BF16, name=f"rounded{c}", align_bytes=64) for c in range(PICKS)]
-        codes = [keep.tile([P, J], U32, name=f"codes{c}", align_bytes=64) for c in range(PICKS)]
-        scales = [keep.tile([P, J], U8, name=f"scales{c}", align_bytes=64) for c in range(PICKS)]
-        first = [keep.tile([P, MT * CH], F32, name=f"first{q}") for q in range(NCH)]
-        pooled2 = [keep.tile([P, MT * CH], F32, name=f"pooled2_{q}") for q in range(NCH)]
-        pooled3 = [keep.tile([P, MT * CH], F32, name=f"pooled3_{q}") for q in range(NCH)]
-        result = [keep.tile([P, MT, CH], F32, name=f"result{q}") for q in range(NCH)]
+        early = keep.tile([P, 2, ENTRIES], F32, name="early")
+        cells = [keep.tile([P, 2, HALF], F32, name=f"cell{k}") for k in range(4)]
+        rounded = keep.tile([P, ENTRIES, PACK], BF16, name="rounded", align_bytes=64)
+        codes = keep.tile([P, ENTRIES], U32, name="codes", align_bytes=64)
+        scales = keep.tile([P, ENTRIES], U8, name="scales", align_bytes=64)
+        first = [keep.tile([P, MT, HALF], F32, name=f"first{h}") for h in range(2)]
+        pooled2 = [keep.tile([P, MT, HALF], F32, name=f"pooled2_{h}") for h in range(2)]
+        pooled3 = [keep.tile([P, MT, HALF], F32, name=f"pooled3_{h}") for h in range(2)]
+        result = [keep.tile([P, MT, HALF], F32, name=f"result{h}") for h in range(2)]
+        banks = [psum.tile([P, 2, HALF], F32, name=f"bank{k}") for k in range(8)]
         out_view = out.rearrange("(m p) j -> p m j", p=P)
-        acc = {}
 
-        def gather(dst, t, c, j0, width):
-            col = (c * J + j0) // GROUP
-            nc.vector.tensor_tensor(
-                dst, planes[t][:].indirect(offsets[:, col : col + width // GROUP]), weights[c][:, j0 : j0 + width], MULT
+        def entries(i):
+            h, c = PIECES[i]
+            return slice(c * J + h * HALF, c * J + (h + 1) * HALF)
+
+        def gather(dst, t, cols):
+            lists = offsets[:, cols.start // GROUP : cols.stop // GROUP]
+            nc.vector.tensor_tensor(dst, planes[t][:].indirect(lists), weights[:, cols], MULT)
+
+        def gather_late(i, t):
+            cell = cells[CELL[i]]
+            gather(cell[:, t - 2, :], t, entries(i))
+            if t == 3:
+                nc.scalar.copy(rounded[:, entries(i), 2:4], cell[:].rearrange("p t j -> p j t"))
+
+        def quantize(i):
+            cols = entries(i)
+            nc.vector.quantize_mx(
+                out=codes[:, cols].bitcast(FP8X4),
+                scales=scales[:, cols],
+                in_=rounded[:, cols, :].rearrange("p j t -> p (j t)"),
             )
 
-        def gather2(h, c):
-            gather(late[h, c][:, 0, :], 2, c, 2 * h * CH, 2 * CH)
-
-        def gather3(q, c):
-            s = slice(q % 2 * CH, (q % 2 + 1) * CH)
-            gather(late[q // 2, c][:, 1, s], 3, c, q * CH, CH)
-            nc.scalar.copy(rounded[c][:, q * CH : (q + 1) * CH, 2:4], late[q // 2, c][:, :, s].rearrange("p t j -> p j t"))
-
-        def project(q):
-            cols = slice(q * CH, (q + 1) * CH)
-            for c in range(PICKS):
-                nc.vector.quantize_mx(
-                    out=codes[c][:, cols].bitcast(FP8X4),
-                    scales=scales[c][:, cols],
-                    in_=rounded[c][:, cols, :].rearrange("p j t -> p (j t)"),
+        def project(i):
+            h, c = PIECES[i]
+            cols = entries(i)
+            for m in range(MT):
+                nc.tensor.matmul_mx(
+                    out=banks[BANKS[i] + m // 2][:, m % 2, :],
+                    lhsT=w_codes[:, 2 * m * P : 2 * (m + 1) * P].bitcast(FP4X4),
+                    lhsT_scale=w_plane[:, m * P : (m + 1) * P],
+                    rhs=codes[:, cols].bitcast(FP8X4),
+                    rhs_scale=scales[:, cols],
+                    start=True,
+                    stop=True,
                 )
-                acc[q, c] = psum.tile([P, MT * CH], F32, name=f"acc{c}", bufs=2 if c == 0 else 3)
-                for m in range(MT):
-                    nc.tensor.matmul_mx(
-                        out=acc[q, c][:, m * CH : (m + 1) * CH],
-                        lhsT=w_codes[:, 2 * m * P : 2 * (m + 1) * P].bitcast(FP4X4),
-                        lhsT_scale=w_plane[:, m * P : (m + 1) * P],
-                        rhs=codes[c][:, cols].bitcast(FP8X4),
-                        rhs_scale=scales[c][:, cols],
-                        start=True,
-                        stop=True,
-                    )
+            for k in range(2):
+                bank = banks[BANKS[i] + k]
                 if c == 0:
-                    nc.scalar.copy(first[q][:], acc[q, 0][:])
+                    nc.scalar.copy(first[h][:, 2 * k : 2 * k + 2, :], bank[:])
+                if c == 1:
+                    nc.vector.tensor_tensor(pooled2[h][:, 2 * k : 2 * k + 2, :], bank[:], first[h][:, 2 * k : 2 * k + 2, :], MAX)
 
-        def max_a(q, m0=0, m1=MT):
-            s = slice(m0 * CH, m1 * CH)
-            nc.vector.tensor_tensor(pooled2[q][:, s], acc[q, 1][:, s], first[q][:, s], MAX)
-
-        def max_b(q, m0=0, m1=MT, queue=nc.sync):
-            s = slice(m0 * CH, m1 * CH)
-            nc.vector.tensor_tensor(pooled3[q][:, s], acc[q, 2][:, s], pooled2[q][:, s], MAX)
+        def finish(i, m0, m1, cols, queue):
+            h = PIECES[i][0]
+            bank = banks[BANKS[i] + m0 // 2]
+            nc.vector.tensor_tensor(
+                pooled3[h][:, m0:m1, cols], bank[:, m0 % 2 : m0 % 2 + m1 - m0, cols], pooled2[h][:, m0:m1, cols], MAX
+            )
             for m in range(m0, m1):
-                nc.scalar.activation(result[q][:, m, :], pooled3[q][:, m * CH : (m + 1) * CH], GELU, bias=bias[:, m : m + 1])
-            queue.dma_start(out_view[:, m0:m1, q * CH : (q + 1) * CH], result[q][:, m0:m1, :])
+                nc.scalar.activation(result[h][:, m, cols], pooled3[h][:, m, cols], GELU, bias=bias[:, m : m + 1])
+            queue.dma_start(out_view[:, m0:m1, h * HALF + cols.start : h * HALF + cols.stop], result[h][:, m0:m1, cols])
 
-        gather(early[0][:, 0, 0:HEAD], 0, 0, 0, HEAD)
-        gather(early[0][:, 0, HEAD:J], 0, 0, HEAD, J - HEAD)
-        for c in range(1, PICKS):
-            gather(early[c][:, 0, :], 0, c, 0, J)
+        for cut in cuts:
+            gather(early[:, 0, cut], 0, cut)
         for c in range(PICKS):
-            gather(early[c][:, 1, :], 1, c, 0, J)
-            nc.scalar.copy(rounded[c][:, :, 0:2], early[c][:].rearrange("p t j -> p j t"))
+            cols = slice(c * J, (c + 1) * J)
+            gather(early[:, 1, cols], 1, cols)
+            nc.scalar.copy(rounded[:, cols, 0:2], early[:, :, cols].rearrange("p t j -> p j t"))
+        for t in (2, 3):
+            for i in range(4):
+                gather_late(i, t)
 
-        for c in range(PICKS):
-            gather2(0, c)
-        for c in range(PICKS):
-            gather3(0, c)
-        for c in range(PICKS):
-            gather3(1, c)
-        project(0)
-        for c in range(PICKS):
-            gather2(1, c)
-            gather3(2, c)
-        max_a(0)
-        project(1)
-        max_b(0)
-        gather3(3, 0)
-        project(2)
-        gather3(3, 1)
-        max_a(1)
-        gather3(3, 2)
-        max_b(1)
-        max_a(2)
-        project(3)
-        max_b(2)
-        max_a(3, 0, 2)
-        max_a(3, 2, 4)
-        max_b(3, 0, 2)
-        max_b(3, 2, 3)
-        max_b(3, 3, 4, nc.scalar)
+        quantize(0)
+        gather_late(4, 2)
+        gather_late(4, 3)
+        quantize(1)
+        quantize(2)
+        gather_late(5, 2)
+        gather_late(5, 3)
+        for i in (3, 4, 5):
+            quantize(i)
+
+        for i in range(4):
+            project(i)
+        whole = slice(0, HALF)
+        for k in range(2):
+            finish(2, 2 * k, 2 * k + 2, whole, nc.sync)
+        project(4)
+        project(5)
+        for m in range(MT - 1):
+            finish(5, m, m + 1, whole, nc.sync)
+        finish(5, MT - 1, MT, slice(0, HALF // 2), nc.sync)
+        finish(5, MT - 1, MT, slice(HALF // 2, HALF), nc.scalar)

@@ -24,9 +24,10 @@ GROUP = 16
 HALF = J // 2
 MT = N // P
 ENTRIES = PICKS * J
-FIRST_CUTS = [0, 256, 768, ENTRIES]
+BLOCK = 32
+FIRST_CUTS = [0, 256, 512, ENTRIES]
 PIECES = [(h, c) for h in range(2) for c in range(PICKS)]
-CELL = [0, 1, 2, 3, 0, 2]
+SLOT = [0, 3, 4, 1, 2, 5]
 BANKS = [0, 2, 4, 6, 0, 2]
 
 
@@ -38,7 +39,10 @@ def tile_list_max_gelu_kernel(tc, xT, wgt, w_words, w_scales, b, offs, out):
 
         offsets = keep.tile([P, ENTRIES // GROUP], U16, name="offsets")
         planes = [keep.tile([P, T], F32, name=f"plane{t}") for t in range(PACK)]
-        weights = keep.tile([P, ENTRIES], F32, name="weights")
+        weights = keep.tile([P, ENTRIES], F32, name="weights", align_bytes=64)
+        compact = keep.tile([P, BLOCK], F32, name="compact", align_bytes=64)
+        turned = keep.tile([P, BLOCK], F32, name="turned", align_bytes=64)
+        spread = keep.tile([P, GROUP, 2, GROUP], F32, name="spread", align_bytes=64)
         w_codes = keep.tile([P, 2 * N], U8, name="w_codes", align_bytes=64)
         w_plane = keep.tile([P, N], U8, name="w_plane", align_bytes=64)
         bias = keep.tile([P, MT], F32, name="bias")
@@ -50,10 +54,11 @@ def tile_list_max_gelu_kernel(tc, xT, wgt, w_words, w_scales, b, offs, out):
 
         x_planes = xT.rearrange("(p t) n -> t p n", t=PACK)
         cuts = [slice(lo, hi) for lo, hi in zip(FIRST_CUTS, FIRST_CUTS[1:])]
+        head_rows = wgt.rearrange("(g r) (s c) -> r g s c", r=GROUP, c=BLOCK)[0]
+        nc.sync.dma_start(compact[:], head_rows[:, 0:GROUP, :])
         nc.sync.dma_start(offsets[:], offs)
-        nc.sync.dma_start(weights[:, cuts[0]], wgt[:, cuts[0]])
         nc.sync.dma_start(planes[0][:], x_planes[0])
-        for cut in cuts[1:]:
+        for cut in cuts[2:]:
             nc.sync.dma_start(weights[:, cut], wgt[:, cut])
         for t in range(1, PACK):
             nc.sync.dma_start(planes[t][:], x_planes[t])
@@ -63,9 +68,16 @@ def tile_list_max_gelu_kernel(tc, xT, wgt, w_words, w_scales, b, offs, out):
         with nc.allow_non_contiguous_dma(reason="one bias value a partition"):
             nc.sync.dma_start(bias[:], b.rearrange("(m p) -> p m", p=P))
 
-        early = keep.tile([P, 2, ENTRIES], F32, name="early")
-        cells = [keep.tile([P, 2, HALF], F32, name=f"cell{k}") for k in range(4)]
-        rounded = keep.tile([P, ENTRIES, PACK], BF16, name="rounded", align_bytes=64)
+        nc.vector.transpose(turned[:], compact[:])
+        by_chunk = turned[:].rearrange("p (h s) -> p s h", h=2)
+        for n in range(2):
+            chunks = slice(8 * n, 8 * n + 8)
+            nc.vector.tensor_copy(spread[:, chunks], by_chunk[:, chunks, :].unsqueeze(3).to_broadcast([P, 8, 2, GROUP]))
+        for n in range(2):
+            nc.vector.transpose(weights[:, cuts[n]], spread[:, 8 * n : 8 * n + 8].rearrange("p s h r -> p (s h r)"))
+
+        picked = keep.tile([P, PACK, ENTRIES], F32, name="picked")
+        rounded = keep.tile([P, len(PIECES), HALF, PACK], BF16, name="rounded", align_bytes=64)
         codes = keep.tile([P, ENTRIES], U32, name="codes", align_bytes=64)
         scales = keep.tile([P, ENTRIES], U8, name="scales", align_bytes=64)
         first = [keep.tile([P, MT, HALF], F32, name=f"first{h}") for h in range(2)]
@@ -83,23 +95,28 @@ def tile_list_max_gelu_kernel(tc, xT, wgt, w_words, w_scales, b, offs, out):
             lists = offsets[:, cols.start // GROUP : cols.stop // GROUP]
             nc.vector.tensor_tensor(dst, planes[t][:].indirect(lists), weights[:, cols], MULT)
 
-        def gather_late(i, t):
-            cell = cells[CELL[i]]
-            gather(cell[:, t - 2, :], t, entries(i))
-            if t == 3:
-                nc.scalar.copy(rounded[:, entries(i), 2:4], cell[:].rearrange("p t j -> p j t"))
+        def stored(i, count=1):
+            return slice(SLOT[i] * HALF, (SLOT[i] + count) * HALF)
 
-        def quantize(i):
-            cols = entries(i)
+        def round_pair(src, t, slots):
+            nc.scalar.copy(rounded[:, slots, :, t : t + 2], src.rearrange("p t (n j) -> p n j t", j=HALF))
+
+        def gather_late(i, t, home):
+            gather(picked[:, t, entries(home)], t, entries(i))
+            if t == 3:
+                round_pair(picked[:, 2:4, entries(home)], 2, slice(SLOT[i], SLOT[i] + 1))
+
+        def quantize(i, count=1):
+            cols = stored(i, count)
             nc.vector.quantize_mx(
                 out=codes[:, cols].bitcast(FP8X4),
                 scales=scales[:, cols],
-                in_=rounded[:, cols, :].rearrange("p j t -> p (j t)"),
+                in_=rounded[:, SLOT[i] : SLOT[i] + count].rearrange("p n j t -> p (n j t)"),
             )
 
         def project(i):
             h, c = PIECES[i]
-            cols = entries(i)
+            cols = stored(i)
             for m in range(MT):
                 nc.tensor.matmul_mx(
                     out=banks[BANKS[i] + m // 2][:, m % 2, :],
@@ -127,27 +144,31 @@ def tile_list_max_gelu_kernel(tc, xT, wgt, w_words, w_scales, b, offs, out):
                 nc.scalar.activation(result[h][:, m, cols], pooled3[h][:, m, cols], GELU, bias=bias[:, m : m + 1])
             queue.dma_start(out_view[:, m0:m1, h * HALF + cols.start : h * HALF + cols.stop], result[h][:, m0:m1, cols])
 
-        for cut in cuts:
-            gather(early[:, 0, cut], 0, cut)
-        for c in range(PICKS):
-            cols = slice(c * J, (c + 1) * J)
-            gather(early[:, 1, cols], 1, cols)
-            nc.scalar.copy(rounded[:, cols, 0:2], early[:, :, cols].rearrange("p t j -> p j t"))
-        for t in (2, 3):
-            for i in range(4):
-                gather_late(i, t)
-
+        for cols in (slice(0, J), slice(J, ENTRIES)):
+            gather(picked[:, 0, cols], 0, cols)
+        for cols in (slice(0, HALF), slice(HALF, 3 * HALF), slice(3 * HALF, ENTRIES)):
+            gather(picked[:, 1, cols], 1, cols)
+        round_pair(picked[:, 0:2, 0:HALF], 0, slice(0, 1))
+        round_pair(picked[:, 0:2, HALF : 3 * HALF], 0, slice(1, 4, 2))
+        round_pair(picked[:, 0:2, 3 * HALF : 5 * HALF], 0, slice(2, 5, 2))
+        gather(picked[:, 2, 0 : 3 * HALF], 2, slice(0, 3 * HALF))
+        gather_late(0, 3, 0)
+        gather_late(1, 3, 1)
+        gather_late(2, 2, 5)
+        gather_late(2, 3, 5)
         quantize(0)
-        gather_late(4, 2)
-        gather_late(4, 3)
-        quantize(1)
-        quantize(2)
-        gather_late(5, 2)
-        gather_late(5, 3)
-        for i in (3, 4, 5):
-            quantize(i)
+        gather_late(3, 3, 3)
+        gather_late(4, 2, 0)
+        gather_late(4, 3, 0)
+        quantize(1, 2)
+        for t in (2, 3):
+            gather(picked[:, t, entries(5)], t, entries(5))
+        quantize(3, 2)
 
-        for i in range(4):
+        project(0)
+        nc.scalar.copy(rounded[:, SLOT[5]], picked[:, :, entries(5)].rearrange("p t j -> p j t"))
+        quantize(5)
+        for i in range(1, 4):
             project(i)
         whole = slice(0, HALF)
         for k in range(2):

@@ -151,6 +151,7 @@ def tile_list_max_gelu_kernel(tc, xT, wgt, w_words, w_scales, b, offs, out):
         round_pair(picked[:, 0:2, 0:HALF], 0, slice(0, 1))
         round_pair(picked[:, 0:2, HALF : 3 * HALF], 0, slice(1, 4, 2))
         round_pair(picked[:, 0:2, 3 * HALF : 5 * HALF], 0, slice(2, 5, 2))
+        round_pair(picked[:, 0:2, 5 * HALF :], 0, slice(5, 6))
         gather(picked[:, 2, 0 : 3 * HALF], 2, slice(0, 3 * HALF))
         gather_late(0, 3, 0)
         gather_late(1, 3, 1)
@@ -161,12 +162,12 @@ def tile_list_max_gelu_kernel(tc, xT, wgt, w_words, w_scales, b, offs, out):
         gather_late(4, 2, 0)
         gather_late(4, 3, 0)
         quantize(1, 2)
-        for t in (2, 3):
-            gather(picked[:, t, entries(5)], t, entries(5))
+        gather(picked[:, 2, entries(5)], 2, entries(5))
+        gather(picked[:, 3, entries(5)], 3, entries(5))
         quantize(3, 2)
 
         project(0)
-        nc.scalar.copy(rounded[:, SLOT[5]], picked[:, :, entries(5)].rearrange("p t j -> p j t"))
+        round_pair(picked[:, 2:4, entries(5)], 2, slice(5, 6))
         quantize(5)
         for i in range(1, 4):
             project(i)

@@ -24,8 +24,7 @@ GROUP = 16
 HALF = J // 2
 MT = N // P
 ENTRIES = PICKS * J
-BLOCK = 32
-FIRST_CUTS = [0, 256, 512, ENTRIES]
+FIRST_CUTS = [0, 256, 768, ENTRIES]
 PIECES = [(h, c) for h in range(2) for c in range(PICKS)]
 SLOT = [0, 3, 4, 1, 2, 5]
 BANKS = [0, 2, 4, 6, 0, 2]
@@ -40,9 +39,6 @@ def tile_list_max_gelu_kernel(tc, xT, wgt, w_words, w_scales, b, offs, out):
         offsets = keep.tile([P, ENTRIES // GROUP], U16, name="offsets")
         planes = [keep.tile([P, T], F32, name=f"plane{t}") for t in range(PACK)]
         weights = keep.tile([P, ENTRIES], F32, name="weights", align_bytes=64)
-        compact = keep.tile([P, BLOCK], F32, name="compact", align_bytes=64)
-        turned = keep.tile([P, BLOCK], F32, name="turned", align_bytes=64)
-        spread = keep.tile([P, GROUP, 2, GROUP], F32, name="spread", align_bytes=64)
         w_codes = keep.tile([P, 2 * N], U8, name="w_codes", align_bytes=64)
         w_plane = keep.tile([P, N], U8, name="w_plane", align_bytes=64)
         bias = keep.tile([P, MT], F32, name="bias")
@@ -54,11 +50,10 @@ def tile_list_max_gelu_kernel(tc, xT, wgt, w_words, w_scales, b, offs, out):
 
         x_planes = xT.rearrange("(p t) n -> t p n", t=PACK)
         cuts = [slice(lo, hi) for lo, hi in zip(FIRST_CUTS, FIRST_CUTS[1:])]
-        head_rows = wgt.rearrange("(g r) (s c) -> r g s c", r=GROUP, c=BLOCK)[0]
-        nc.sync.dma_start(compact[:], head_rows[:, 0:GROUP, :])
         nc.sync.dma_start(offsets[:], offs)
+        nc.sync.dma_start(weights[:, cuts[0]], wgt[:, cuts[0]])
         nc.sync.dma_start(planes[0][:], x_planes[0])
-        for cut in cuts[2:]:
+        for cut in cuts[1:]:
             nc.sync.dma_start(weights[:, cut], wgt[:, cut])
         for t in range(1, PACK):
             nc.sync.dma_start(planes[t][:], x_planes[t])
@@ -67,14 +62,6 @@ def tile_list_max_gelu_kernel(tc, xT, wgt, w_words, w_scales, b, offs, out):
             nc.sync.dma_start(w_plane[32 * q : 32 * q + 4, :].bitcast(I32), w_scales[0, 4 * q : 4 * q + 4, :].bitcast(I32))
         with nc.allow_non_contiguous_dma(reason="one bias value a partition"):
             nc.sync.dma_start(bias[:], b.rearrange("(m p) -> p m", p=P))
-
-        nc.vector.transpose(turned[:], compact[:])
-        by_chunk = turned[:].rearrange("p (h s) -> p s h", h=2)
-        for n in range(2):
-            chunks = slice(8 * n, 8 * n + 8)
-            nc.vector.tensor_copy(spread[:, chunks], by_chunk[:, chunks, :].unsqueeze(3).to_broadcast([P, 8, 2, GROUP]))
-        for n in range(2):
-            nc.vector.transpose(weights[:, cuts[n]], spread[:, 8 * n : 8 * n + 8].rearrange("p s h r -> p (s h r)"))
 
         picked = keep.tile([P, PACK, ENTRIES], F32, name="picked")
         rounded = keep.tile([P, len(PIECES), HALF, PACK], BF16, name="rounded", align_bytes=64)
@@ -144,7 +131,7 @@ def tile_list_max_gelu_kernel(tc, xT, wgt, w_words, w_scales, b, offs, out):
                 nc.scalar.activation(result[h][:, m, cols], pooled3[h][:, m, cols], GELU, bias=bias[:, m : m + 1])
             queue.dma_start(out_view[:, m0:m1, h * HALF + cols.start : h * HALF + cols.stop], result[h][:, m0:m1, cols])
 
-        for cols in (slice(0, J), slice(J, ENTRIES)):
+        for cols in cuts:
             gather(picked[:, 0, cols], 0, cols)
         for cols in (slice(0, HALF), slice(HALF, 3 * HALF), slice(3 * HALF, ENTRIES)):
             gather(picked[:, 1, cols], 1, cols)

@@ -131,15 +131,16 @@ def tile_list_max_gelu_kernel(tc, xT, wgt, w_words, w_scales, b, offs, out):
                 nc.scalar.activation(result[h][:, m, cols], pooled3[h][:, m, cols], GELU, bias=bias[:, m : m + 1])
             queue.dma_start(out_view[:, m0:m1, h * HALF + cols.start : h * HALF + cols.stop], result[h][:, m0:m1, cols])
 
-        for cols in cuts:
-            gather(picked[:, 0, cols], 0, cols)
-        for cols in (slice(0, HALF), slice(HALF, 3 * HALF), slice(3 * HALF, ENTRIES)):
-            gather(picked[:, 1, cols], 1, cols)
+        short = (slice(0, HALF), slice(HALF, 3 * HALF), slice(3 * HALF, 5 * HALF), slice(5 * HALF, ENTRIES))
+        for t in range(2):
+            for cols in short:
+                gather(picked[:, t, cols], t, cols)
         round_pair(picked[:, 0:2, 0:HALF], 0, slice(0, 1))
         round_pair(picked[:, 0:2, HALF : 3 * HALF], 0, slice(1, 4, 2))
         round_pair(picked[:, 0:2, 3 * HALF : 5 * HALF], 0, slice(2, 5, 2))
         round_pair(picked[:, 0:2, 5 * HALF :], 0, slice(5, 6))
-        gather(picked[:, 2, 0 : 3 * HALF], 2, slice(0, 3 * HALF))
+        for cols in short[:2]:
+            gather(picked[:, 2, cols], 2, cols)
         gather_late(0, 3, 0)
         gather_late(1, 3, 1)
         gather_late(2, 2, 5)

@@ -55,11 +55,12 @@ def tile_list_max_gelu_kernel(tc, xT, wgt, w_words, w_scales, b, offs, out):
         nc.sync.dma_start(planes[0][:], x_planes[0])
         for cut in cuts[1:]:
             nc.sync.dma_start(weights[:, cut], wgt[:, cut])
-        for t in range(1, PACK):
-            nc.sync.dma_start(planes[t][:], x_planes[t])
+        nc.sync.dma_start(planes[1][:], x_planes[1])
         nc.sync.dma_start(w_codes[:].bitcast(I32), w_words[0].bitcast(I32))
         for q in range(4):
             nc.sync.dma_start(w_plane[32 * q : 32 * q + 4, :].bitcast(I32), w_scales[0, 4 * q : 4 * q + 4, :].bitcast(I32))
+        for t in range(2, PACK):
+            nc.sync.dma_start(planes[t][:], x_planes[t])
         with nc.allow_non_contiguous_dma(reason="one bias value a partition"):
             nc.sync.dma_start(bias[:], b.rearrange("(m p) -> p m", p=P))
 

@@ -24,10 +24,7 @@ GROUP = 16
 HALF = J // 2
 MT = N // P
 ENTRIES = PICKS * J
-FIRST_CUTS = [0, 256, 768, ENTRIES]
-PIECES = [(h, c) for h in range(2) for c in range(PICKS)]
-SLOT = [0, 3, 4, 1, 2, 5]
-BANKS = [0, 2, 4, 6, 0, 2]
+RUNS = [slice(0, HALF), slice(HALF, 3 * HALF), slice(3 * HALF, 5 * HALF), slice(5 * HALF, ENTRIES)]
 
 
 def tile_list_max_gelu_kernel(tc, xT, wgt, w_words, w_scales, b, offs, out):
@@ -39,6 +36,7 @@ def tile_list_max_gelu_kernel(tc, xT, wgt, w_words, w_scales, b, offs, out):
         offsets = keep.tile([P, ENTRIES // GROUP], U16, name="offsets")
         planes = [keep.tile([P, T], F32, name=f"plane{t}") for t in range(PACK)]
         weights = keep.tile([P, ENTRIES], F32, name="weights", align_bytes=64)
+        ones = keep.tile([P, HALF], F32, name="ones")
         w_codes = keep.tile([P, 2 * N], U8, name="w_codes", align_bytes=64)
         w_plane = keep.tile([P, N], U8, name="w_plane", align_bytes=64)
         bias = keep.tile([P, MT], F32, name="bias")
@@ -47,15 +45,15 @@ def tile_list_max_gelu_kernel(tc, xT, wgt, w_words, w_scales, b, offs, out):
         nc.vector.memset(warm[:, 0:1], 0.0)
         nc.scalar.activation(warm[:, 1:2], warm[:, 0:1], GELU)
         nc.vector.memset(w_plane[:].bitcast(I32), 0)
+        nc.vector.memset(ones[:], 1.0)
 
         x_planes = xT.rearrange("(p t) n -> t p n", t=PACK)
-        cuts = [slice(lo, hi) for lo, hi in zip(FIRST_CUTS, FIRST_CUTS[1:])]
         nc.sync.dma_start(offsets[:], offs)
-        nc.sync.dma_start(weights[:, cuts[0]], wgt[:, cuts[0]])
         nc.sync.dma_start(planes[0][:], x_planes[0])
-        for cut in cuts[1:]:
-            nc.sync.dma_start(weights[:, cut], wgt[:, cut])
+        for run in RUNS[:3]:
+            nc.sync.dma_start(weights[:, run], wgt[:, run])
         nc.sync.dma_start(planes[1][:], x_planes[1])
+        nc.sync.dma_start(weights[:, RUNS[3]], wgt[:, RUNS[3]])
         nc.sync.dma_start(w_codes[:].bitcast(I32), w_words[0].bitcast(I32))
         for q in range(4):
             nc.sync.dma_start(w_plane[32 * q : 32 * q + 4, :].bitcast(I32), w_scales[0, 4 * q : 4 * q + 4, :].bitcast(I32))
@@ -64,50 +62,39 @@ def tile_list_max_gelu_kernel(tc, xT, wgt, w_words, w_scales, b, offs, out):
         with nc.allow_non_contiguous_dma(reason="one bias value a partition"):
             nc.sync.dma_start(bias[:], b.rearrange("(m p) -> p m", p=P))
 
-        picked = keep.tile([P, PACK, ENTRIES], F32, name="picked")
-        rounded = keep.tile([P, len(PIECES), HALF, PACK], BF16, name="rounded", align_bytes=64)
+        def width(run):
+            return run.stop - run.start
+
+        plain = keep.tile([P, HALF], F32, name="plain")
+        early = keep.tile([P, 2, RUNS[2].stop], F32, name="early")
+        cells = keep.tile([P, 10, HALF], F32, name="cells")
+        rounded = [keep.tile([P, width(run), PACK], BF16, name=f"rounded{r}", align_bytes=64) for r, run in enumerate(RUNS)]
         codes = keep.tile([P, ENTRIES], U32, name="codes", align_bytes=64)
         scales = keep.tile([P, ENTRIES], U8, name="scales", align_bytes=64)
-        first = [keep.tile([P, MT, HALF], F32, name=f"first{h}") for h in range(2)]
-        pooled2 = [keep.tile([P, MT, HALF], F32, name=f"pooled2_{h}") for h in range(2)]
-        pooled3 = [keep.tile([P, MT, HALF], F32, name=f"pooled3_{h}") for h in range(2)]
-        result = [keep.tile([P, MT, HALF], F32, name=f"result{h}") for h in range(2)]
         banks = [psum.tile([P, 2, HALF], F32, name=f"bank{k}") for k in range(8)]
         out_view = out.rearrange("(m p) j -> p m j", p=P)
 
-        def entries(i):
-            h, c = PIECES[i]
-            return slice(c * J + h * HALF, c * J + (h + 1) * HALF)
-
-        def gather(dst, t, cols):
+        def gather(dst, t, cols, factor):
             lists = offsets[:, cols.start // GROUP : cols.stop // GROUP]
-            nc.vector.tensor_tensor(dst, planes[t][:].indirect(lists), weights[:, cols], MULT)
+            nc.vector.tensor_tensor(dst, planes[t][:].indirect(lists), factor, MULT)
 
-        def stored(i, count=1):
-            return slice(SLOT[i] * HALF, (SLOT[i] + count) * HALF)
+        def round_pair(r, t, src):
+            nc.scalar.copy(rounded[r][:, :, t : t + 2], src.rearrange("p t j -> p j t"))
 
-        def round_pair(src, t, slots):
-            nc.scalar.copy(rounded[:, slots, :, t : t + 2], src.rearrange("p t (n j) -> p n j t", j=HALF))
-
-        def gather_late(i, t, home):
-            gather(picked[:, t, entries(home)], t, entries(i))
-            if t == 3:
-                round_pair(picked[:, 2:4, entries(home)], 2, slice(SLOT[i], SLOT[i] + 1))
-
-        def quantize(i, count=1):
-            cols = stored(i, count)
+        def quantize(r, lo=0, hi=None):
+            hi = width(RUNS[r]) if hi is None else hi
+            cols = slice(RUNS[r].start + lo, RUNS[r].start + hi)
             nc.vector.quantize_mx(
                 out=codes[:, cols].bitcast(FP8X4),
                 scales=scales[:, cols],
-                in_=rounded[:, SLOT[i] : SLOT[i] + count].rearrange("p n j t -> p (n j t)"),
+                in_=rounded[r][:, lo:hi, :].rearrange("p j t -> p (j t)"),
             )
 
-        def project(i):
-            h, c = PIECES[i]
-            cols = stored(i)
+        def project(h, c, bank):
+            cols = slice(c * J + h * HALF, c * J + (h + 1) * HALF)
             for m in range(MT):
                 nc.tensor.matmul_mx(
-                    out=banks[BANKS[i] + m // 2][:, m % 2, :],
+                    out=banks[bank + m // 2][:, m % 2, :],
                     lhsT=w_codes[:, 2 * m * P : 2 * (m + 1) * P].bitcast(FP4X4),
                     lhsT_scale=w_plane[:, m * P : (m + 1) * P],
                     rhs=codes[:, cols].bitcast(FP8X4),
@@ -115,57 +102,77 @@ def tile_list_max_gelu_kernel(tc, xT, wgt, w_words, w_scales, b, offs, out):
                     start=True,
                     stop=True,
                 )
-            for k in range(2):
-                bank = banks[BANKS[i] + k]
-                if c == 0:
-                    nc.scalar.copy(first[h][:, 2 * k : 2 * k + 2, :], bank[:])
-                if c == 1:
-                    nc.vector.tensor_tensor(pooled2[h][:, 2 * k : 2 * k + 2, :], bank[:], first[h][:, 2 * k : 2 * k + 2, :], MAX)
 
-        def finish(i, m0, m1, cols, queue):
-            h = PIECES[i][0]
-            bank = banks[BANKS[i] + m0 // 2]
-            nc.vector.tensor_tensor(
-                pooled3[h][:, m0:m1, cols], bank[:, m0 % 2 : m0 % 2 + m1 - m0, cols], pooled2[h][:, m0:m1, cols], MAX
-            )
+        def flat(bank):
+            return banks[bank][:].rearrange("p m j -> p (m j)")
+
+        def cell(first, count=1):
+            return cells[:, first : first + count, :].rearrange("p n j -> p (n j)")
+
+        def fetch(dst, t, r):
+            gather(dst, t, RUNS[r], weights[:, RUNS[r]])
+
+        gather(plain[:], 0, RUNS[3], ones[:])
+        for t in range(2):
+            for r in range(3):
+                fetch(early[:, t, RUNS[r]], t, r)
+        for r in range(3):
+            round_pair(r, 0, early[:, :, RUNS[r]])
+
+        for t in range(2):
+            fetch(cell(2 * t), 2 + t, 0)
+            fetch(cell(6 + 2 * t, 2), 2 + t, 1)
+        round_pair(0, 2, cells[:, 0:3:2, :])
+        round_pair(1, 2, cell(6, 4).rearrange("p (t j) -> p t j", t=2))
+
+        first = [[cell(4, 2), early[:, 0, 0:J]], [early[:, 1, 0:J], early[:, 1, J : 2 * J]]]
+        fetch(cell(0, 2), 2, 2)
+        quantize(0)
+        fetch(cell(2, 2), 3, 2)
+        project(0, 0, 0)
+        nc.scalar.copy(first[0][0], flat(0))
+        round_pair(2, 2, cell(0, 4).rearrange("p (t j) -> p t j", t=2))
+        nc.scalar.copy(first[0][1], flat(1))
+
+        fetch(cell(6), 1, 3)
+        quantize(1)
+        fetch(cell(7), 2, 3)
+        fetch(cell(8), 3, 3)
+        project(0, 1, 4)
+        project(1, 0, 2)
+        round_pair(3, 2, cells[:, 7:9, :])
+        nc.scalar.copy(first[1][0], flat(2))
+
+        pooled = [[cell(0, 2), cell(2, 2)], [early[:, 0, J : 2 * J], cell(8, 2)]]
+        nc.vector.tensor_tensor(pooled[0][0], flat(4), first[0][0], MAX)
+        nc.gpsimd.tensor_tensor(cell(5), plain[:], weights[:, RUNS[3]], MULT)
+        round_pair(3, 0, cells[:, 5:7, :])
+        nc.scalar.copy(first[1][1], flat(3))
+        quantize(2, HALF, J)
+        quantize(2, 0, HALF)
+        nc.vector.tensor_tensor(pooled[0][1], flat(5), first[0][1], MAX)
+        project(0, 2, 6)
+        project(1, 1, 0)
+
+        top = [keep.tile([P, MT, HALF], F32, name=f"top{h}") for h in range(2)]
+        result = [keep.tile([P, MT, HALF], F32, name=f"result{h}") for h in range(2)]
+
+        def finish(h, bank, m0, m1, cols, queue):
+            two = pooled[h][m0 // 2].rearrange("p (m j) -> p m j", j=HALF)
+            rows = slice(m0 % 2, m0 % 2 + m1 - m0)
+            nc.vector.tensor_tensor(top[h][:, m0:m1, cols], banks[bank + m0 // 2][:, rows, cols], two[:, rows, cols], MAX)
             for m in range(m0, m1):
-                nc.scalar.activation(result[h][:, m, cols], pooled3[h][:, m, cols], GELU, bias=bias[:, m : m + 1])
+                nc.scalar.activation(result[h][:, m, cols], top[h][:, m, cols], GELU, bias=bias[:, m : m + 1])
             queue.dma_start(out_view[:, m0:m1, h * HALF + cols.start : h * HALF + cols.stop], result[h][:, m0:m1, cols])
 
-        short = (slice(0, HALF), slice(HALF, 3 * HALF), slice(3 * HALF, 5 * HALF), slice(5 * HALF, ENTRIES))
-        for t in range(2):
-            for cols in short:
-                gather(picked[:, t, cols], t, cols)
-        round_pair(picked[:, 0:2, 0:HALF], 0, slice(0, 1))
-        round_pair(picked[:, 0:2, HALF : 3 * HALF], 0, slice(1, 4, 2))
-        round_pair(picked[:, 0:2, 3 * HALF : 5 * HALF], 0, slice(2, 5, 2))
-        round_pair(picked[:, 0:2, 5 * HALF :], 0, slice(5, 6))
-        for cols in short[:2]:
-            gather(picked[:, 2, cols], 2, cols)
-        gather_late(0, 3, 0)
-        gather_late(1, 3, 1)
-        gather_late(2, 2, 5)
-        gather_late(2, 3, 5)
-        quantize(0)
-        gather_late(3, 3, 3)
-        gather_late(4, 2, 0)
-        gather_late(4, 3, 0)
-        quantize(1, 2)
-        gather(picked[:, 2, entries(5)], 2, entries(5))
-        gather(picked[:, 3, entries(5)], 3, entries(5))
-        quantize(3, 2)
-
-        project(0)
-        round_pair(picked[:, 2:4, entries(5)], 2, slice(5, 6))
-        quantize(5)
-        for i in range(1, 4):
-            project(i)
         whole = slice(0, HALF)
         for k in range(2):
-            finish(2, 2 * k, 2 * k + 2, whole, nc.sync)
-        project(4)
-        project(5)
+            finish(0, 6, 2 * k, 2 * k + 2, whole, nc.sync)
+        quantize(3)
+        project(1, 2, 2)
+        for k in range(2):
+            nc.vector.tensor_tensor(pooled[1][k], flat(k), first[1][k], MAX)
         for m in range(MT - 1):
-            finish(5, m, m + 1, whole, nc.sync)
-        finish(5, MT - 1, MT, slice(0, HALF // 2), nc.sync)
-        finish(5, MT - 1, MT, slice(HALF // 2, HALF), nc.scalar)
+            finish(1, 2, m, m + 1, whole, nc.sync)
+        finish(1, 2, 3, 4, slice(0, HALF // 2), nc.sync)
+        finish(1, 2, 3, 4, slice(HALF // 2, HALF), nc.scalar)

@@ -36,7 +36,6 @@ def tile_list_max_gelu_kernel(tc, xT, wgt, w_words, w_scales, b, offs, out):
         offsets = keep.tile([P, ENTRIES // GROUP], U16, name="offsets")
         planes = [keep.tile([P, T], F32, name=f"plane{t}") for t in range(PACK)]
         weights = keep.tile([P, ENTRIES], F32, name="weights", align_bytes=64)
-        ones = keep.tile([P, HALF], F32, name="ones")
         w_codes = keep.tile([P, 2 * N], U8, name="w_codes", align_bytes=64)
         w_plane = keep.tile([P, N], U8, name="w_plane", align_bytes=64)
         bias = keep.tile([P, MT], F32, name="bias")
@@ -45,15 +44,14 @@ def tile_list_max_gelu_kernel(tc, xT, wgt, w_words, w_scales, b, offs, out):
         nc.vector.memset(warm[:, 0:1], 0.0)
         nc.scalar.activation(warm[:, 1:2], warm[:, 0:1], GELU)
         nc.vector.memset(w_plane[:].bitcast(I32), 0)
-        nc.vector.memset(ones[:], 1.0)
 
         x_planes = xT.rearrange("(p t) n -> t p n", t=PACK)
         nc.sync.dma_start(offsets[:], offs)
+        nc.sync.dma_start(weights[:, RUNS[0]], wgt[:, RUNS[0]])
         nc.sync.dma_start(planes[0][:], x_planes[0])
-        for run in RUNS[:3]:
-            nc.sync.dma_start(weights[:, run], wgt[:, run])
+        nc.sync.dma_start(weights[:, RUNS[1]], wgt[:, RUNS[1]])
+        nc.sync.dma_start(weights[:, RUNS[2].start :], wgt[:, RUNS[2].start :])
         nc.sync.dma_start(planes[1][:], x_planes[1])
-        nc.sync.dma_start(weights[:, RUNS[3]], wgt[:, RUNS[3]])
         nc.sync.dma_start(w_codes[:].bitcast(I32), w_words[0].bitcast(I32))
         for q in range(4):
             nc.sync.dma_start(w_plane[32 * q : 32 * q + 4, :].bitcast(I32), w_scales[0, 4 * q : 4 * q + 4, :].bitcast(I32))
@@ -65,7 +63,7 @@ def tile_list_max_gelu_kernel(tc, xT, wgt, w_words, w_scales, b, offs, out):
         def width(run):
             return run.stop - run.start
 
-        plain = keep.tile([P, HALF], F32, name="plain")
+        first00 = keep.tile([P, J], F32, name="first00")
         early = keep.tile([P, 2, RUNS[2].stop], F32, name="early")
         cells = keep.tile([P, 10, HALF], F32, name="cells")
         rounded = [keep.tile([P, width(run), PACK], BF16, name=f"rounded{r}", align_bytes=64) for r, run in enumerate(RUNS)]
@@ -112,10 +110,11 @@ def tile_list_max_gelu_kernel(tc, xT, wgt, w_words, w_scales, b, offs, out):
         def fetch(dst, t, r):
             gather(dst, t, RUNS[r], weights[:, RUNS[r]])
 
-        gather(plain[:], 0, RUNS[3], ones[:])
-        for t in range(2):
-            for r in range(3):
-                fetch(early[:, t, RUNS[r]], t, r)
+        for r in range(3):
+            fetch(early[:, 0, RUNS[r]], 0, r)
+        fetch(cell(5), 0, 3)
+        for r in range(3):
+            fetch(early[:, 1, RUNS[r]], 1, r)
         for r in range(3):
             round_pair(r, 0, early[:, :, RUNS[r]])
 
@@ -125,7 +124,7 @@ def tile_list_max_gelu_kernel(tc, xT, wgt, w_words, w_scales, b, offs, out):
         round_pair(0, 2, cells[:, 0:3:2, :])
         round_pair(1, 2, cell(6, 4).rearrange("p (t j) -> p t j", t=2))
 
-        first = [[cell(4, 2), early[:, 0, 0:J]], [early[:, 1, 0:J], early[:, 1, J : 2 * J]]]
+        first = [[first00[:], early[:, 0, 0:J]], [early[:, 1, 0:J], early[:, 1, J : 2 * J]]]
         fetch(cell(0, 2), 2, 2)
         quantize(0)
         fetch(cell(2, 2), 3, 2)
@@ -140,13 +139,12 @@ def tile_list_max_gelu_kernel(tc, xT, wgt, w_words, w_scales, b, offs, out):
         fetch(cell(8), 3, 3)
         project(0, 1, 4)
         project(1, 0, 2)
+        round_pair(3, 0, cells[:, 5:7, :])
         round_pair(3, 2, cells[:, 7:9, :])
         nc.scalar.copy(first[1][0], flat(2))
 
         pooled = [[cell(0, 2), cell(2, 2)], [early[:, 0, J : 2 * J], cell(8, 2)]]
         nc.vector.tensor_tensor(pooled[0][0], flat(4), first[0][0], MAX)
-        nc.gpsimd.tensor_tensor(cell(5), plain[:], weights[:, RUNS[3]], MULT)
-        round_pair(3, 0, cells[:, 5:7, :])
         nc.scalar.copy(first[1][1], flat(3))
         quantize(2, HALF, J)
         quantize(2, 0, HALF)

@@ -76,8 +76,8 @@ def tile_list_max_gelu_kernel(tc, xT, wgt, w_words, w_scales, b, offs, out):
             lists = offsets[:, cols.start // GROUP : cols.stop // GROUP]
             nc.vector.tensor_tensor(dst, planes[t][:].indirect(lists), factor, MULT)
 
-        def round_pair(r, t, src):
-            nc.scalar.copy(rounded[r][:, :, t : t + 2], src.rearrange("p t j -> p j t"))
+        def round_pair(r, t, src, lo=0):
+            nc.scalar.copy(rounded[r][:, lo : lo + src.shape[2], t : t + 2], src.rearrange("p t j -> p j t"))
 
         def quantize(r, lo=0, hi=None):
             hi = width(RUNS[r]) if hi is None else hi
@@ -107,47 +107,53 @@ def tile_list_max_gelu_kernel(tc, xT, wgt, w_words, w_scales, b, offs, out):
         def cell(first, count=1):
             return cells[:, first : first + count, :].rearrange("p n j -> p (n j)")
 
+        last_start = 6 * HALF - 3 * HALF // 2
+        last = cell(0, 10)[:, last_start : last_start + PACK * HALF].rearrange("p (t j) -> p t j", t=PACK)
+
         def fetch(dst, t, r):
             gather(dst, t, RUNS[r], weights[:, RUNS[r]])
 
         for r in range(3):
             fetch(early[:, 0, RUNS[r]], 0, r)
-        fetch(cell(5), 0, 3)
+        fetch(last[:, 0, :], 0, 3)
         for r in range(3):
             fetch(early[:, 1, RUNS[r]], 1, r)
         for r in range(3):
             round_pair(r, 0, early[:, :, RUNS[r]])
 
         for t in range(2):
-            fetch(cell(2 * t), 2 + t, 0)
+            fetch(cell(t), 2 + t, 0)
             fetch(cell(6 + 2 * t, 2), 2 + t, 1)
-        round_pair(0, 2, cells[:, 0:3:2, :])
-        round_pair(1, 2, cell(6, 4).rearrange("p (t j) -> p t j", t=2))
+        fetch(cell(2, 2), 3, 2)
+        round_pair(0, 2, cells[:, 0:2, :])
+        round_pair(1, 2, cells[:, 7:10:2, :], HALF)
+        round_pair(1, 2, cells[:, 6:9:2, :])
 
         first = [[first00[:], early[:, 0, 0:J]], [early[:, 1, 0:J], early[:, 1, J : 2 * J]]]
-        fetch(cell(0, 2), 2, 2)
         quantize(0)
-        fetch(cell(2, 2), 3, 2)
+        fetch(cell(0, 2), 2, 2)
         project(0, 0, 0)
         nc.scalar.copy(first[0][0], flat(0))
         round_pair(2, 2, cell(0, 4).rearrange("p (t j) -> p t j", t=2))
         nc.scalar.copy(first[0][1], flat(1))
 
-        fetch(cell(6), 1, 3)
-        quantize(1)
-        fetch(cell(7), 2, 3)
-        fetch(cell(8), 3, 3)
+        quantize(1, HALF, J)
         project(0, 1, 4)
+        fetch(last[:, 1, :], 1, 3)
+        quantize(1, 0, HALF)
         project(1, 0, 2)
-        round_pair(3, 0, cells[:, 5:7, :])
-        round_pair(3, 2, cells[:, 7:9, :])
-        nc.scalar.copy(first[1][0], flat(2))
+        for t in range(2, PACK):
+            fetch(last[:, t, :], t, 3)
+        for t in (0, 2):
+            round_pair(3, t, last[:, t : t + 2, :])
+        for k in range(2):
+            nc.scalar.copy(first[1][k], flat(2 + k))
 
         pooled = [[cell(0, 2), cell(2, 2)], [early[:, 0, J : 2 * J], cell(8, 2)]]
-        nc.vector.tensor_tensor(pooled[0][0], flat(4), first[0][0], MAX)
-        nc.scalar.copy(first[1][1], flat(3))
+        nc.vector.tensor_tensor(cell(0), banks[4][:, 0, :], first00[:, 0:HALF], MAX)
         quantize(2, HALF, J)
         quantize(2, 0, HALF)
+        nc.vector.tensor_tensor(cell(1), banks[4][:, 1, :], first00[:, HALF:J], MAX)
         nc.vector.tensor_tensor(pooled[0][1], flat(5), first[0][1], MAX)
         project(0, 2, 6)
         project(1, 1, 0)
@@ -164,10 +170,10 @@ def tile_list_max_gelu_kernel(tc, xT, wgt, w_words, w_scales, b, offs, out):
             queue.dma_start(out_view[:, m0:m1, h * HALF + cols.start : h * HALF + cols.stop], result[h][:, m0:m1, cols])
 
         whole = slice(0, HALF)
-        for k in range(2):
-            finish(0, 6, 2 * k, 2 * k + 2, whole, nc.sync)
+        finish(0, 6, 0, 2, whole, nc.sync)
         quantize(3)
         project(1, 2, 2)
+        finish(0, 6, 2, 4, whole, nc.sync)
         for k in range(2):
             nc.vector.tensor_tensor(pooled[1][k], flat(k), first[1][k], MAX)
         for m in range(MT - 1):

@@ -52,11 +52,11 @@ def tile_list_max_gelu_kernel(tc, xT, wgt, w_words, w_scales, b, offs, out):
         nc.sync.dma_start(weights[:, RUNS[1]], wgt[:, RUNS[1]])
         nc.sync.dma_start(weights[:, RUNS[2].start :], wgt[:, RUNS[2].start :])
         nc.sync.dma_start(planes[1][:], x_planes[1])
-        nc.sync.dma_start(w_codes[:].bitcast(I32), w_words[0].bitcast(I32))
         for q in range(4):
             nc.sync.dma_start(w_plane[32 * q : 32 * q + 4, :].bitcast(I32), w_scales[0, 4 * q : 4 * q + 4, :].bitcast(I32))
         for t in range(2, PACK):
             nc.sync.dma_start(planes[t][:], x_planes[t])
+        nc.sync.dma_start(w_codes[:].bitcast(I32), w_words[0].bitcast(I32))
         with nc.allow_non_contiguous_dma(reason="one bias value a partition"):
             nc.sync.dma_start(bias[:], b.rearrange("(m p) -> p m", p=P))
 

@@ -25,6 +25,7 @@ HALF = J // 2
 MT = N // P
 ENTRIES = PICKS * J
 RUNS = [slice(0, HALF), slice(HALF, 3 * HALF), slice(3 * HALF, 5 * HALF), slice(5 * HALF, ENTRIES)]
+CELLS = 10
 
 
 def tile_list_max_gelu_kernel(tc, xT, wgt, w_words, w_scales, b, offs, out):
@@ -65,7 +66,7 @@ def tile_list_max_gelu_kernel(tc, xT, wgt, w_words, w_scales, b, offs, out):
 
         first00 = keep.tile([P, J], F32, name="first00")
         early = keep.tile([P, 2, RUNS[2].stop], F32, name="early")
-        cells = keep.tile([P, 10, HALF], F32, name="cells")
+        cells = keep.tile([P, CELLS, HALF], F32, name="cells")
         rounded = [keep.tile([P, width(run), PACK], BF16, name=f"rounded{r}", align_bytes=64) for r, run in enumerate(RUNS)]
         codes = keep.tile([P, ENTRIES], U32, name="codes", align_bytes=64)
         scales = keep.tile([P, ENTRIES], U8, name="scales", align_bytes=64)
@@ -108,7 +109,7 @@ def tile_list_max_gelu_kernel(tc, xT, wgt, w_words, w_scales, b, offs, out):
             return cells[:, first : first + count, :].rearrange("p n j -> p (n j)")
 
         last_start = 6 * HALF - 3 * HALF // 2
-        last = cell(0, 10)[:, last_start : last_start + PACK * HALF].rearrange("p (t j) -> p t j", t=PACK)
+        last = cell(0, CELLS)[:, last_start : last_start + PACK * HALF].rearrange("p (t j) -> p t j", t=PACK)
 
         def fetch(dst, t, r):
             gather(dst, t, RUNS[r], weights[:, RUNS[r]])
@@ -144,8 +145,9 @@ def tile_list_max_gelu_kernel(tc, xT, wgt, w_words, w_scales, b, offs, out):
         project(1, 0, 2)
         for t in range(2, PACK):
             fetch(last[:, t, :], t, 3)
-        for t in (0, 2):
-            round_pair(3, t, last[:, t : t + 2, :])
+        nc.scalar.copy(
+            rounded[3][:].rearrange("p (c i) t -> p c t i", i=2), last.rearrange("p t (c i) -> p c t i", i=2)
+        )
         for k in range(2):
             nc.scalar.copy(first[1][k], flat(2 + k))
 

from contextlib import ExitStack

import concourse.mybir as mybir

K, N, T, J = 512, 512, 2048, 512
PICKS = 3
FLOPS = 2 * K * N * J * PICKS

F32 = mybir.dt.float32
BF16 = mybir.dt.bfloat16
I32 = mybir.dt.int32
U32 = mybir.dt.uint32
U16 = mybir.dt.uint16
U8 = mybir.dt.uint8
FP8X4 = mybir.dt.float8_e4m3fn_x4
FP4X4 = mybir.dt.float4_e2m1fn_x4
MULT = mybir.AluOpType.mult
MAX = mybir.AluOpType.max
GELU = mybir.ActivationFunctionType.Gelu_apprx_tanh

P = 128
PACK = 4
GROUP = 16
HALF = J // 2
MT = N // P
ENTRIES = PICKS * J
RUNS = [slice(0, HALF), slice(HALF, 3 * HALF), slice(3 * HALF, 5 * HALF), slice(5 * HALF, ENTRIES)]
CELLS = 10


def tile_list_max_gelu_kernel(tc, xT, wgt, w_words, w_scales, b, offs, out):
    nc = tc.nc
    with ExitStack() as ctx:
        keep = ctx.enter_context(tc.tile_pool(name="keep", bufs=1))
        psum = ctx.enter_context(tc.psum_pool(name="psum", bufs=1))

        offsets = keep.tile([P, ENTRIES // GROUP], U16, name="offsets")
        planes = [keep.tile([P, T], F32, name=f"plane{t}") for t in range(PACK)]
        weights = keep.tile([P, ENTRIES], F32, name="weights", align_bytes=64)
        w_codes = keep.tile([P, 2 * N], U8, name="w_codes", align_bytes=64)
        w_plane = keep.tile([P, N], U8, name="w_plane", align_bytes=64)
        bias = keep.tile([P, MT], F32, name="bias")
        warm = keep.tile([P, 2], F32, name="warm")

        nc.vector.memset(warm[:, 0:1], 0.0)
        nc.scalar.activation(warm[:, 1:2], warm[:, 0:1], GELU)
        nc.vector.memset(w_plane[:].bitcast(I32), 0)

        x_planes = xT.rearrange("(p t) n -> t p n", t=PACK)
        nc.sync.dma_start(offsets[:], offs)
        nc.sync.dma_start(weights[:, RUNS[0]], wgt[:, RUNS[0]])
        nc.sync.dma_start(planes[0][:], x_planes[0])
        nc.sync.dma_start(weights[:, RUNS[1]], wgt[:, RUNS[1]])
        nc.sync.dma_start(weights[:, RUNS[2].start :], wgt[:, RUNS[2].start :])
        nc.sync.dma_start(planes[1][:], x_planes[1])
        for q in range(4):
            nc.sync.dma_start(w_plane[32 * q : 32 * q + 4, :].bitcast(I32), w_scales[0, 4 * q : 4 * q + 4, :].bitcast(I32))
        for t in range(2, PACK):
            nc.sync.dma_start(planes[t][:], x_planes[t])
        nc.sync.dma_start(w_codes[:].bitcast(I32), w_words[0].bitcast(I32))
        with nc.allow_non_contiguous_dma(reason="one bias value a partition"):
            nc.sync.dma_start(bias[:], b.rearrange("(m p) -> p m", p=P))

        def width(run):
            return run.stop - run.start

        first00 = keep.tile([P, J], F32, name="first00")
        early = keep.tile([P, 2, RUNS[2].stop], F32, name="early")
        cells = keep.tile([P, CELLS, HALF], F32, name="cells")
        rounded = [keep.tile([P, width(run), PACK], BF16, name=f"rounded{r}", align_bytes=64) for r, run in enumerate(RUNS)]
        codes = keep.tile([P, ENTRIES], U32, name="codes", align_bytes=64)
        scales = keep.tile([P, ENTRIES], U8, name="scales", align_bytes=64)
        banks = [psum.tile([P, 2, HALF], F32, name=f"bank{k}") for k in range(8)]
        out_view = out.rearrange("(m p) j -> p m j", p=P)

        def gather(dst, t, cols, factor):
            lists = offsets[:, cols.start // GROUP : cols.stop // GROUP]
            nc.vector.tensor_tensor(dst, planes[t][:].indirect(lists), factor, MULT)

        def round_pair(r, t, src, lo=0):
            nc.scalar.copy(rounded[r][:, lo : lo + src.shape[2], t : t + 2], src.rearrange("p t j -> p j t"))

        def quantize(r, lo=0, hi=None):
            hi = width(RUNS[r]) if hi is None else hi
            cols = slice(RUNS[r].start + lo, RUNS[r].start + hi)
            nc.vector.quantize_mx(
                out=codes[:, cols].bitcast(FP8X4),
                scales=scales[:, cols],
                in_=rounded[r][:, lo:hi, :].rearrange("p j t -> p (j t)"),
            )

        def project(h, c, bank):
            cols = slice(c * J + h * HALF, c * J + (h + 1) * HALF)
            for m in range(MT):
                nc.tensor.matmul_mx(
                    out=banks[bank + m // 2][:, m % 2, :],
                    lhsT=w_codes[:, 2 * m * P : 2 * (m + 1) * P].bitcast(FP4X4),
                    lhsT_scale=w_plane[:, m * P : (m + 1) * P],
                    rhs=codes[:, cols].bitcast(FP8X4),
                    rhs_scale=scales[:, cols],
                    start=True,
                    stop=True,
                )

        def flat(bank):
            return banks[bank][:].rearrange("p m j -> p (m j)")

        def cell(first, count=1):
            return cells[:, first : first + count, :].rearrange("p n j -> p (n j)")

        last_start = 6 * HALF - 3 * HALF // 2
        last = cell(0, CELLS)[:, last_start : last_start + PACK * HALF].rearrange("p (t j) -> p t j", t=PACK)

        def fetch(dst, t, r):
            gather(dst, t, RUNS[r], weights[:, RUNS[r]])

        for r in range(3):
            fetch(early[:, 0, RUNS[r]], 0, r)
        fetch(last[:, 0, :], 0, 3)
        for r in range(3):
            fetch(early[:, 1, RUNS[r]], 1, r)
        for r in range(3):
            round_pair(r, 0, early[:, :, RUNS[r]])

        for t in range(2):
            fetch(cell(t), 2 + t, 0)
            fetch(cell(6 + 2 * t, 2), 2 + t, 1)
        fetch(cell(2, 2), 3, 2)
        round_pair(0, 2, cells[:, 0:2, :])
        round_pair(1, 2, cells[:, 7:10:2, :], HALF)
        round_pair(1, 2, cells[:, 6:9:2, :])

        first = [[first00[:], early[:, 0, 0:J]], [early[:, 1, 0:J], early[:, 1, J : 2 * J]]]
        quantize(0)
        fetch(cell(0, 2), 2, 2)
        project(0, 0, 0)
        nc.scalar.copy(first[0][0], flat(0))
        round_pair(2, 2, cell(0, 4).rearrange("p (t j) -> p t j", t=2))
        nc.scalar.copy(first[0][1], flat(1))

        quantize(1, HALF, J)
        project(0, 1, 4)
        fetch(last[:, 1, :], 1, 3)
        quantize(1, 0, HALF)
        project(1, 0, 2)
        for t in range(2, PACK):
            fetch(last[:, t, :], t, 3)
        nc.scalar.copy(
            rounded[3][:].rearrange("p (c i) t -> p c t i", i=2), last.rearrange("p t (c i) -> p c t i", i=2)
        )
        for k in range(2):
            nc.scalar.copy(first[1][k], flat(2 + k))

        pooled = [[cell(0, 2), cell(2, 2)], [early[:, 0, J : 2 * J], cell(8, 2)]]
        nc.vector.tensor_tensor(cell(0), banks[4][:, 0, :], first00[:, 0:HALF], MAX)
        quantize(2, HALF, J)
        quantize(2, 0, HALF)
        nc.vector.tensor_tensor(cell(1), banks[4][:, 1, :], first00[:, HALF:J], MAX)
        nc.vector.tensor_tensor(pooled[0][1], flat(5), first[0][1], MAX)
        project(0, 2, 6)
        project(1, 1, 0)

        top = [keep.tile([P, MT, HALF], F32, name=f"top{h}") for h in range(2)]
        result = [keep.tile([P, MT, HALF], F32, name=f"result{h}") for h in range(2)]

        def finish(h, bank, m0, m1, cols, queue):
            two = pooled[h][m0 // 2].rearrange("p (m j) -> p m j", j=HALF)
            rows = slice(m0 % 2, m0 % 2 + m1 - m0)
            nc.vector.tensor_tensor(top[h][:, m0:m1, cols], banks[bank + m0 // 2][:, rows, cols], two[:, rows, cols], MAX)
            for m in range(m0, m1):
                nc.scalar.activation(result[h][:, m, cols], top[h][:, m, cols], GELU, bias=bias[:, m : m + 1])
            queue.dma_start(out_view[:, m0:m1, h * HALF + cols.start : h * HALF + cols.stop], result[h][:, m0:m1, cols])

        whole = slice(0, HALF)
        finish(0, 6, 0, 2, whole, nc.sync)
        quantize(3)
        project(1, 2, 2)
        finish(0, 6, 2, 4, whole, nc.sync)
        for k in range(2):
            nc.vector.tensor_tensor(pooled[1][k], flat(k), first[1][k], MAX)
        for m in range(MT - 1):
            finish(1, 2, m, m + 1, whole, nc.sync)
        finish(1, 2, 3, 4, slice(0, HALF // 2), nc.sync)
        finish(1, 2, 3, 4, slice(HALF // 2, HALF), nc.scalar)
